import numpy as np
import ml_dtypes

BF16 = ml_dtypes.bfloat16


def bf(x):
    return np.asarray(x, np.float32).astype(BF16)


def f32(x):
    return np.asarray(x, np.float32)


def f64(x):
    return np.asarray(x).astype(np.float64)


def striped(idx):
    return np.tile(idx.reshape(-1, 16).T, (8, 1))


S, K, M, N, E, Q = 512, 512, 128, 1024, 4, 256


def two_experts():
    first = np.random.permutation(S).reshape(E, S // E)
    return np.concatenate([np.random.permutation(np.concatenate([first[e], first[(e + 1) % E]])) for e in range(E)])


def setup_inputs():
    return {"table": bf(np.random.standard_normal((K, S))), "w": bf(np.random.standard_normal((E, K, M)) / np.sqrt(K)), "c": f32(0.2 + 0.8 * np.random.random_sample((1, N))), "offs": striped(two_experts())}


def reference(table, w, c, offs):
    idx = offs[:16].T.reshape(-1)
    x = f64(table)[:, idx]
    y = np.concatenate([f64(w)[e].T @ x[:, e * Q : (e + 1) * Q] for e in range(E)], axis=1)
    return y * f64(c)

@@ -1,0 +1,56 @@
+import concourse.mybir as mybir
+
+P = 128
+S = 512
+K = 512
+KB = K // P
+M = 128
+E = 4
+Q = 256
+N = E * Q
+QC = Q // 16
+
+FLOPS = 2 * K * M * N
+
+BF16, F32, U16 = mybir.dt.bfloat16, mybir.dt.float32, mybir.dt.uint16
+MULT = mybir.AluOpType.mult
+
+
+def tile_gather_matmul_kernel(tc, table, w, c, offs, out):
+    nc = tc.nc
+    with (
+        tc.tile_pool(name="held", bufs=1) as held,
+        tc.psum_pool(name="psum", bufs=1) as psum,
+    ):
+        offsets = held.tile([P, N // 16], U16, name="offsets")
+        nc.sync.dma_start(offsets[:], offs)
+
+        blocks = []
+        for b in range(KB):
+            block = held.tile([P, S], BF16, name=f"block{b}")
+            nc.sync.dma_start(block[:], table[b * P : (b + 1) * P, :])
+            blocks.append(block)
+
+        weights = []
+        for e in range(E):
+            matrix = held.tile([P, KB, M], BF16, name=f"matrix{e}")
+            nc.scalar.dma_start(matrix[:], w[e].rearrange("(b p) m -> p b m", p=P))
+            weights.append(matrix)
+
+        gains = held.tile([P, N], F32, name="gains")
+        nc.gpsimd.dma_start(gains[:], c.rearrange("o n -> (o n)").partition_broadcast(P))
+
+        for e in range(E):
+            piece = offsets[:, e * QC : (e + 1) * QC]
+            bank = psum.tile([P, Q], F32, name=f"bank{e}")
+            for b in range(KB):
+                nc.tensor.matmul(
+                    bank[:],
+                    weights[e][:, b, :],
+                    blocks[b][:].indirect(piece),
+                    start=(b == 0),
+                    stop=(b == KB - 1),
+                )
+            scaled = held.tile([P, Q], F32, name=f"scaled{e}")
+            nc.vector.tensor_tensor(scaled[:], bank[:], gains[:, e * Q : (e + 1) * Q], MULT)
+            nc.sync.dma_start(out[:, e * Q : (e + 1) * Q], scaled[:])

@@ -10,6 +10,8 @@ Q = 256
 N = E * Q
 QC = Q // 16
 
+WARM = 20
+
 FLOPS = 2 * K * M * N
 
 BF16, F32, U16 = mybir.dt.bfloat16, mybir.dt.float32, mybir.dt.uint16
@@ -25,20 +27,29 @@ def tile_gather_matmul_kernel(tc, table, w, c, offs, out):
         offsets = held.tile([P, N // 16], U16, name="offsets")
         nc.sync.dma_start(offsets[:], offs)
 
+        table_by_block = table.rearrange("(p b) s -> b p s", b=KB)
         blocks = []
         for b in range(KB):
             block = held.tile([P, S], BF16, name=f"block{b}")
-            nc.sync.dma_start(block[:], table[b * P : (b + 1) * P, :])
+            nc.sync.dma_start(block[:], table_by_block[b])
             blocks.append(block)
 
+        router = c.rearrange("o n -> (o n)")
         weights = []
+        gains = []
         for e in range(E):
             matrix = held.tile([P, KB, M], BF16, name=f"matrix{e}")
-            nc.scalar.dma_start(matrix[:], w[e].rearrange("(b p) m -> p b m", p=P))
+            nc.scalar.dma_start(matrix[:], w[e].rearrange("(p b) m -> p b m", b=KB))
             weights.append(matrix)
+            gain = held.tile([P, Q], F32, name=f"gain{e}")
+            nc.scalar.dma_start(gain[:], router[e * Q : (e + 1) * Q].partition_broadcast(P))
+            gains.append(gain)
 
-        gains = held.tile([P, N], F32, name="gains")
-        nc.gpsimd.dma_start(gains[:], c.rearrange("o n -> (o n)").partition_broadcast(P))
+        zeros = held.tile([P, M], BF16, name="zeros")
+        nc.gpsimd.memset(zeros[:], 0.0)
+        idle_bank = psum.tile([P, M], F32, name="idle_bank")
+        for i in range(WARM):
+            nc.tensor.matmul(idle_bank[:], zeros[:], zeros[:], start=True, stop=True)
 
         for e in range(E):
             piece = offsets[:, e * QC : (e + 1) * QC]
@@ -52,5 +63,5 @@ def tile_gather_matmul_kernel(tc, table, w, c, offs, out):
                     stop=(b == KB - 1),
                 )
             scaled = held.tile([P, Q], F32, name=f"scaled{e}")
-            nc.vector.tensor_tensor(scaled[:], bank[:], gains[:, e * Q : (e + 1) * Q], MULT)
+            nc.vector.tensor_tensor(scaled[:], bank[:], gains[e][:], MULT)
             nc.sync.dma_start(out[:, e * Q : (e + 1) * Q], scaled[:])

@@ -24,8 +24,13 @@ def tile_gather_matmul_kernel(tc, table, w, c, offs, out):
         tc.tile_pool(name="held", bufs=1) as held,
         tc.psum_pool(name="psum", bufs=1) as psum,
     ):
+
         offsets = held.tile([P, N // 16], U16, name="offsets")
         nc.sync.dma_start(offsets[:], offs)
+
+        weights = held.tile([P, E, KB, M], BF16, name="weights")
+        w_by_partition = w.rearrange("e (p b) m -> p e b m", b=KB)
+        nc.sync.dma_start(weights[:, 0:1], w_by_partition[:, 0:1])
 
         table_by_block = table.rearrange("(p b) s -> b p s", b=KB)
         blocks = []
@@ -34,16 +39,10 @@ def tile_gather_matmul_kernel(tc, table, w, c, offs, out):
             nc.sync.dma_start(block[:], table_by_block[b])
             blocks.append(block)
 
-        router = c.rearrange("o n -> (o n)")
-        weights = []
-        gains = []
-        for e in range(E):
-            matrix = held.tile([P, KB, M], BF16, name=f"matrix{e}")
-            nc.scalar.dma_start(matrix[:], w[e].rearrange("(p b) m -> p b m", b=KB))
-            weights.append(matrix)
-            gain = held.tile([P, Q], F32, name=f"gain{e}")
-            nc.scalar.dma_start(gain[:], router[e * Q : (e + 1) * Q].partition_broadcast(P))
-            gains.append(gain)
+        nc.sync.dma_start(weights[:, 1:E], w_by_partition[:, 1:E])
+
+        gains = held.tile([P, N], F32, name="gains")
+        nc.sync.dma_start(gains[:], c.rearrange("o n -> (o n)").partition_broadcast(P))
 
         zeros = held.tile([P, M], BF16, name="zeros")
         nc.gpsimd.memset(zeros[:], 0.0)
@@ -57,11 +56,11 @@ def tile_gather_matmul_kernel(tc, table, w, c, offs, out):
             for b in range(KB):
                 nc.tensor.matmul(
                     bank[:],
-                    weights[e][:, b, :],
+                    weights[:, e, b, :],
                     blocks[b][:].indirect(piece),
                     start=(b == 0),
                     stop=(b == KB - 1),
                 )
             scaled = held.tile([P, Q], F32, name=f"scaled{e}")
-            nc.vector.tensor_tensor(scaled[:], bank[:], gains[e][:], MULT)
+            nc.vector.tensor_tensor(scaled[:], bank[:], gains[:, e * Q : (e + 1) * Q], MULT)
             nc.sync.dma_start(out[:, e * Q : (e + 1) * Q], scaled[:])

@@ -42,7 +42,7 @@ def tile_gather_matmul_kernel(tc, table, w, c, offs, out):
         nc.sync.dma_start(weights[:, 1:E], w_by_partition[:, 1:E])
 
         gains = held.tile([P, N], F32, name="gains")
-        nc.sync.dma_start(gains[:], c.rearrange("o n -> (o n)").partition_broadcast(P))
+        nc.scalar.dma_start(gains[:], c.rearrange("o n -> (o n)").partition_broadcast(P))
 
         zeros = held.tile([P, M], BF16, name="zeros")
         nc.gpsimd.memset(zeros[:], 0.0)

@@ -8,6 +8,7 @@ M = 128
 E = 4
 Q = 256
 N = E * Q
+T = 32
 QC = Q // 16
 
 WARM = 20
@@ -33,22 +34,28 @@ def tile_gather_matmul_kernel(tc, table, w, c, offs, out):
         nc.sync.dma_start(weights[:, 0:1], w_by_partition[:, 0:1])
 
         table_by_block = table.rearrange("(p b) s -> b p s", b=KB)
-        blocks = []
+        blocks = [held.tile([P, S], BF16, name=f"block{b}") for b in range(KB)]
         for b in range(KB):
-            block = held.tile([P, S], BF16, name=f"block{b}")
-            nc.sync.dma_start(block[:], table_by_block[b])
-            blocks.append(block)
+            nc.sync.dma_start(blocks[b][:], table_by_block[b])
+
+        rows = held.tile([P, N], F32, name="rows", align_bytes=64)
+        nc.vector.memset(rows[:], 0.0)
+        nc.sync.dma_start(rows[0:P:T, :], c.rearrange("o n -> (o n)").partition_broadcast(P // T))
 
         nc.sync.dma_start(weights[:, 1:E], w_by_partition[:, 1:E])
-
-        gains = held.tile([P, N], F32, name="gains")
-        nc.scalar.dma_start(gains[:], c.rearrange("o n -> (o n)").partition_broadcast(P))
 
         zeros = held.tile([P, M], BF16, name="zeros")
         nc.gpsimd.memset(zeros[:], 0.0)
         idle_bank = psum.tile([P, M], F32, name="idle_bank")
         for i in range(WARM):
             nc.tensor.matmul(idle_bank[:], zeros[:], zeros[:], start=True, stop=True)
+
+        turned = held.tile([P, N // T, T], F32, name="turned", align_bytes=64)
+        nc.vector.transpose(turned[:].rearrange("p a r -> p (a r)"), rows[:])
+        spread = held.tile([P, N // T, T], F32, name="spread", align_bytes=64)
+        nc.vector.tensor_copy(spread[:], turned[:, :, 0:1].to_broadcast([P, N // T, T]))
+        gains = held.tile([P, N], F32, name="gains", align_bytes=64)
+        nc.vector.transpose(gains[:], spread[:].rearrange("p a r -> p (a r)"))
 
         for e in range(E):
             piece = offsets[:, e * QC : (e + 1) * QC]

@@ -11,7 +11,7 @@ N = E * Q
 T = 32
 QC = Q // 16
 
-WARM = 20
+WARM = 10
 
 FLOPS = 2 * K * M * N
 
@@ -29,6 +29,11 @@ def tile_gather_matmul_kernel(tc, table, w, c, offs, out):
         offsets = held.tile([P, N // 16], U16, name="offsets")
         nc.sync.dma_start(offsets[:], offs)
 
+        folded = held.tile([P, T], F32, name="folded", align_bytes=64)
+        c_rows = c.rearrange("o (a r) -> (o a) r", r=T)
+        for g in range(P // T):
+            nc.scalar.dma_start(folded[g * T : (g + 1) * T, :], c_rows)
+
         weights = held.tile([P, E, KB, M], BF16, name="weights")
         w_by_partition = w.rearrange("e (p b) m -> p e b m", b=KB)
         nc.sync.dma_start(weights[:, 0:1], w_by_partition[:, 0:1])
@@ -38,11 +43,8 @@ def tile_gather_matmul_kernel(tc, table, w, c, offs, out):
         for b in range(KB):
             nc.sync.dma_start(blocks[b][:], table_by_block[b])
 
-        rows = held.tile([P, N], F32, name="rows", align_bytes=64)
-        nc.vector.memset(rows[:], 0.0)
-        nc.sync.dma_start(rows[0:P:T, :], c.rearrange("o n -> (o n)").partition_broadcast(P // T))
-
-        nc.sync.dma_start(weights[:, 1:E], w_by_partition[:, 1:E])
+        for e in range(1, E):
+            nc.sync.dma_start(weights[:, e : e + 1], w_by_partition[:, e : e + 1])
 
         zeros = held.tile([P, M], BF16, name="zeros")
         nc.gpsimd.memset(zeros[:], 0.0)
@@ -50,10 +52,10 @@ def tile_gather_matmul_kernel(tc, table, w, c, offs, out):
         for i in range(WARM):
             nc.tensor.matmul(idle_bank[:], zeros[:], zeros[:], start=True, stop=True)
 
-        turned = held.tile([P, N // T, T], F32, name="turned", align_bytes=64)
-        nc.vector.transpose(turned[:].rearrange("p a r -> p (a r)"), rows[:])
+        turned = held.tile([P, N // T], F32, name="turned", align_bytes=64)
+        nc.vector.transpose(turned[:], folded[:])
         spread = held.tile([P, N // T, T], F32, name="spread", align_bytes=64)
-        nc.vector.tensor_copy(spread[:], turned[:, :, 0:1].to_broadcast([P, N // T, T]))
+        nc.vector.tensor_copy(spread[:], turned[:].unsqueeze(2).to_broadcast([P, N // T, T]))
         gains = held.tile([P, N], F32, name="gains", align_bytes=64)
         nc.vector.transpose(gains[:], spread[:].rearrange("p a r -> p (a r)"))
 

@@ -11,8 +11,6 @@ N = E * Q
 T = 32
 QC = Q // 16
 
-WARM = 10
-
 FLOPS = 2 * K * M * N
 
 BF16, F32, U16 = mybir.dt.bfloat16, mybir.dt.float32, mybir.dt.uint16
@@ -45,12 +43,6 @@ def tile_gather_matmul_kernel(tc, table, w, c, offs, out):
 
         for e in range(1, E):
             nc.sync.dma_start(weights[:, e : e + 1], w_by_partition[:, e : e + 1])
-
-        zeros = held.tile([P, M], BF16, name="zeros")
-        nc.gpsimd.memset(zeros[:], 0.0)
-        idle_bank = psum.tile([P, M], F32, name="idle_bank")
-        for i in range(WARM):
-            nc.tensor.matmul(idle_bank[:], zeros[:], zeros[:], start=True, stop=True)
 
         turned = held.tile([P, N // T], F32, name="turned", align_bytes=64)
         nc.vector.transpose(turned[:], folded[:])

@@ -63,5 +63,10 @@ def tile_gather_matmul_kernel(tc, table, w, c, offs, out):
                     stop=(b == KB - 1),
                 )
             scaled = held.tile([P, Q], F32, name=f"scaled{e}")
-            nc.vector.tensor_tensor(scaled[:], bank[:], gains[:, e * Q : (e + 1) * Q], MULT)
-            nc.sync.dma_start(out[:, e * Q : (e + 1) * Q], scaled[:])
+            width = Q // 2 if e == E - 1 else Q
+            for first in range(0, Q, width):
+                columns = slice(e * Q + first, e * Q + first + width)
+                nc.vector.tensor_tensor(
+                    scaled[:, first : first + width], bank[:, first : first + width], gains[:, columns], MULT
+                )
+                nc.sync.dma_start(out[:, columns], scaled[:, first : first + width])

@@ -29,8 +29,7 @@ def tile_gather_matmul_kernel(tc, table, w, c, offs, out):
 
         folded = held.tile([P, T], F32, name="folded", align_bytes=64)
         c_rows = c.rearrange("o (a r) -> (o a) r", r=T)
-        for g in range(P // T):
-            nc.scalar.dma_start(folded[g * T : (g + 1) * T, :], c_rows)
+        nc.scalar.dma_start(folded[:], c_rows.partition_broadcast(P // T))
 
         weights = held.tile([P, E, KB, M], BF16, name="weights")
         w_by_partition = w.rearrange("e (p b) m -> p e b m", b=KB)

@@ -27,10 +27,6 @@ def tile_gather_matmul_kernel(tc, table, w, c, offs, out):
         offsets = held.tile([P, N // 16], U16, name="offsets")
         nc.sync.dma_start(offsets[:], offs)
 
-        folded = held.tile([P, T], F32, name="folded", align_bytes=64)
-        c_rows = c.rearrange("o (a r) -> (o a) r", r=T)
-        nc.scalar.dma_start(folded[:], c_rows.partition_broadcast(P // T))
-
         weights = held.tile([P, E, KB, M], BF16, name="weights")
         w_by_partition = w.rearrange("e (p b) m -> p e b m", b=KB)
         nc.sync.dma_start(weights[:, 0:1], w_by_partition[:, 0:1])
@@ -40,7 +36,13 @@ def tile_gather_matmul_kernel(tc, table, w, c, offs, out):
         for b in range(KB):
             nc.sync.dma_start(blocks[b][:], table_by_block[b])
 
-        for e in range(1, E):
+        nc.sync.dma_start(weights[:, 1:2], w_by_partition[:, 1:2])
+
+        folded = held.tile([P, T], F32, name="folded", align_bytes=64)
+        c_rows = c.rearrange("o (a r) -> (o a) r", r=T)
+        nc.sync.dma_start(folded[:], c_rows.partition_broadcast(P // T))
+
+        for e in range(2, E):
             nc.sync.dma_start(weights[:, e : e + 1], w_by_partition[:, e : e + 1])
 
         turned = held.tile([P, N // T], F32, name="turned", align_bytes=64)

@@ -10,6 +10,7 @@ Q = 256
 N = E * Q
 T = 32
 QC = Q // 16
+ROW_START = 256
 
 FLOPS = 2 * K * M * N
 
@@ -27,12 +28,12 @@ def tile_gather_matmul_kernel(tc, table, w, c, offs, out):
         offsets = held.tile([P, N // 16], U16, name="offsets")
         nc.sync.dma_start(offsets[:], offs)
 
-        weights = held.tile([P, E, KB, M], BF16, name="weights")
+        weights = held.tile([P, E, KB, M], BF16, name="weights", align_bytes=ROW_START)
         w_by_partition = w.rearrange("e (p b) m -> p e b m", b=KB)
         nc.sync.dma_start(weights[:, 0:1], w_by_partition[:, 0:1])
 
         table_by_block = table.rearrange("(p b) s -> b p s", b=KB)
-        blocks = [held.tile([P, S], BF16, name=f"block{b}") for b in range(KB)]
+        blocks = [held.tile([P, S], BF16, name=f"block{b}", align_bytes=ROW_START) for b in range(KB)]
         for b in range(KB):
             nc.sync.dma_start(blocks[b][:], table_by_block[b])
 
@@ -63,7 +64,7 @@ def tile_gather_matmul_kernel(tc, table, w, c, offs, out):
                     start=(b == 0),
                     stop=(b == KB - 1),
                 )
-            scaled = held.tile([P, Q], F32, name=f"scaled{e}")
+            scaled = held.tile([P, Q], F32, name=f"scaled{e}", align_bytes=ROW_START)
             width = Q // 2 if e == E - 1 else Q
             for first in range(0, Q, width):
                 columns = slice(e * Q + first, e * Q + first + width)

@@ -34,10 +34,10 @@ def tile_gather_matmul_kernel(tc, table, w, c, offs, out):
 
         table_by_block = table.rearrange("(p b) s -> b p s", b=KB)
         blocks = [held.tile([P, S], BF16, name=f"block{b}", align_bytes=ROW_START) for b in range(KB)]
-        for b in range(KB):
-            nc.sync.dma_start(blocks[b][:], table_by_block[b])
-
+        nc.sync.dma_start(blocks[0][:], table_by_block[0])
         nc.sync.dma_start(weights[:, 1:2], w_by_partition[:, 1:2])
+        for b in range(1, KB):
+            nc.sync.dma_start(blocks[b][:], table_by_block[b])
 
         folded = held.tile([P, T], F32, name="folded", align_bytes=64)
         c_rows = c.rearrange("o (a r) -> (o a) r", r=T)
@@ -53,22 +53,23 @@ def tile_gather_matmul_kernel(tc, table, w, c, offs, out):
         gains = held.tile([P, N], F32, name="gains", align_bytes=64)
         nc.vector.transpose(gains[:], spread[:].rearrange("p a r -> p (a r)"))
 
-        for e in range(E):
-            piece = offsets[:, e * QC : (e + 1) * QC]
-            bank = psum.tile([P, Q], F32, name=f"bank{e}")
+        banks = [psum.tile([P, Q], F32, name=f"bank{e}") for e in range(E)]
+        for pair in range(0, E, 2):
             for b in range(KB):
-                nc.tensor.matmul(
-                    bank[:],
-                    weights[:, e, b, :],
-                    blocks[b][:].indirect(piece),
-                    start=(b == 0),
-                    stop=(b == KB - 1),
-                )
-            scaled = held.tile([P, Q], F32, name=f"scaled{e}", align_bytes=ROW_START)
-            width = Q // 2 if e == E - 1 else Q
-            for first in range(0, Q, width):
-                columns = slice(e * Q + first, e * Q + first + width)
-                nc.vector.tensor_tensor(
-                    scaled[:, first : first + width], bank[:, first : first + width], gains[:, columns], MULT
-                )
-                nc.sync.dma_start(out[:, columns], scaled[:, first : first + width])
+                for e in (pair, pair + 1):
+                    nc.tensor.matmul(
+                        banks[e][:],
+                        weights[:, e, b, :],
+                        blocks[b][:].indirect(offsets[:, e * QC : (e + 1) * QC]),
+                        start=(b == 0),
+                        stop=(b == KB - 1),
+                    )
+            for e in (pair, pair + 1):
+                scaled = held.tile([P, Q], F32, name=f"scaled{e}", align_bytes=ROW_START)
+                width = Q // 2 if e == E - 1 else Q
+                for first in range(0, Q, width):
+                    columns = slice(e * Q + first, e * Q + first + width)
+                    nc.vector.tensor_tensor(
+                        scaled[:, first : first + width], banks[e][:, first : first + width], gains[:, columns], MULT
+                    )
+                    nc.sync.dma_start(out[:, columns], scaled[:, first : first + width])

@@ -10,6 +10,7 @@ Q = 256
 N = E * Q
 T = 32
 QC = Q // 16
+C_BEFORE = 2
 ROW_START = 256
 
 FLOPS = 2 * K * M * N
@@ -36,13 +37,15 @@ def tile_gather_matmul_kernel(tc, table, w, c, offs, out):
         blocks = [held.tile([P, S], BF16, name=f"block{b}", align_bytes=ROW_START) for b in range(KB)]
         nc.sync.dma_start(blocks[0][:], table_by_block[0])
         nc.sync.dma_start(weights[:, 1:2], w_by_partition[:, 1:2])
-        for b in range(1, KB):
+        for b in range(1, C_BEFORE):
             nc.sync.dma_start(blocks[b][:], table_by_block[b])
 
         folded = held.tile([P, T], F32, name="folded", align_bytes=64)
         c_rows = c.rearrange("o (a r) -> (o a) r", r=T)
         nc.sync.dma_start(folded[:], c_rows.partition_broadcast(P // T))
 
+        for b in range(C_BEFORE, KB):
+            nc.sync.dma_start(blocks[b][:], table_by_block[b])
         for e in range(2, E):
             nc.sync.dma_start(weights[:, e : e + 1], w_by_partition[:, e : e + 1])
 

@@ -52,9 +52,14 @@ def tile_gather_matmul_kernel(tc, table, w, c, offs, out):
         turned = held.tile([P, N // T], F32, name="turned", align_bytes=64)
         nc.vector.transpose(turned[:], folded[:])
         spread = held.tile([P, N // T, T], F32, name="spread", align_bytes=64)
-        nc.vector.tensor_copy(spread[:], turned[:].unsqueeze(2).to_broadcast([P, N // T, T]))
         gains = held.tile([P, N], F32, name="gains", align_bytes=64)
-        nc.vector.transpose(gains[:], spread[:].rearrange("p a r -> p (a r)"))
+        half = N // T // 2
+        for first in (0, half):
+            rows = slice(first, first + half)
+            nc.scalar.copy(spread[:, rows], turned[:, rows].unsqueeze(2).to_broadcast([P, half, T]))
+            nc.vector.transpose(
+                gains[:, first * T : (first + half) * T], spread[:, rows].rearrange("p a r -> p (a r)")
+            )
 
         banks = [psum.tile([P, Q], F32, name=f"bank{e}") for e in range(E)]
         for pair in range(0, E, 2):

@@ -10,7 +10,6 @@ Q = 256
 N = E * Q
 T = 32
 QC = Q // 16
-C_BEFORE = 2
 ROW_START = 256
 
 FLOPS = 2 * K * M * N
@@ -37,15 +36,13 @@ def tile_gather_matmul_kernel(tc, table, w, c, offs, out):
         blocks = [held.tile([P, S], BF16, name=f"block{b}", align_bytes=ROW_START) for b in range(KB)]
         nc.sync.dma_start(blocks[0][:], table_by_block[0])
         nc.sync.dma_start(weights[:, 1:2], w_by_partition[:, 1:2])
-        for b in range(1, C_BEFORE):
+        for b in range(1, KB):
             nc.sync.dma_start(blocks[b][:], table_by_block[b])
 
         folded = held.tile([P, T], F32, name="folded", align_bytes=64)
         c_rows = c.rearrange("o (a r) -> (o a) r", r=T)
         nc.sync.dma_start(folded[:], c_rows.partition_broadcast(P // T))
 
-        for b in range(C_BEFORE, KB):
-            nc.sync.dma_start(blocks[b][:], table_by_block[b])
         for e in range(2, E):
             nc.sync.dma_start(weights[:, e : e + 1], w_by_partition[:, e : e + 1])
 

@@ -10,6 +10,7 @@ Q = 256
 N = E * Q
 T = 32
 QC = Q // 16
+C_BEFORE = 3
 ROW_START = 256
 
 FLOPS = 2 * K * M * N
@@ -36,13 +37,15 @@ def tile_gather_matmul_kernel(tc, table, w, c, offs, out):
         blocks = [held.tile([P, S], BF16, name=f"block{b}", align_bytes=ROW_START) for b in range(KB)]
         nc.sync.dma_start(blocks[0][:], table_by_block[0])
         nc.sync.dma_start(weights[:, 1:2], w_by_partition[:, 1:2])
-        for b in range(1, KB):
+        for b in range(1, C_BEFORE):
             nc.sync.dma_start(blocks[b][:], table_by_block[b])
 
         folded = held.tile([P, T], F32, name="folded", align_bytes=64)
         c_rows = c.rearrange("o (a r) -> (o a) r", r=T)
         nc.sync.dma_start(folded[:], c_rows.partition_broadcast(P // T))
 
+        for b in range(C_BEFORE, KB):
+            nc.sync.dma_start(blocks[b][:], table_by_block[b])
         for e in range(2, E):
             nc.sync.dma_start(weights[:, e : e + 1], w_by_partition[:, e : e + 1])
 
@@ -50,13 +53,10 @@ def tile_gather_matmul_kernel(tc, table, w, c, offs, out):
         nc.vector.transpose(turned[:], folded[:])
         spread = held.tile([P, N // T, T], F32, name="spread", align_bytes=64)
         gains = held.tile([P, N], F32, name="gains", align_bytes=64)
-        half = N // T // 2
-        for first in (0, half):
-            rows = slice(first, first + half)
-            nc.scalar.copy(spread[:, rows], turned[:, rows].unsqueeze(2).to_broadcast([P, half, T]))
-            nc.vector.transpose(
-                gains[:, first * T : (first + half) * T], spread[:, rows].rearrange("p a r -> p (a r)")
-            )
+        for e in range(E):
+            rows = slice(e * (Q // T), (e + 1) * (Q // T))
+            nc.scalar.copy(spread[:, rows], turned[:, rows].unsqueeze(2).to_broadcast([P, Q // T, T]))
+            nc.vector.transpose(gains[:, e * Q : (e + 1) * Q], spread[:, rows].rearrange("p a r -> p (a r)"))
 
         banks = [psum.tile([P, Q], F32, name=f"bank{e}") for e in range(E)]
         for pair in range(0, E, 2):

@@ -31,13 +31,16 @@ def tile_gather_matmul_kernel(tc, table, w, c, offs, out):
 
         weights = held.tile([P, E, KB, M], BF16, name="weights", align_bytes=ROW_START)
         w_by_partition = w.rearrange("e (p b) m -> p e b m", b=KB)
-        nc.sync.dma_start(weights[:, 0:1], w_by_partition[:, 0:1])
 
         table_by_block = table.rearrange("(p b) s -> b p s", b=KB)
         blocks = [held.tile([P, S], BF16, name=f"block{b}", align_bytes=ROW_START) for b in range(KB)]
-        nc.sync.dma_start(blocks[0][:], table_by_block[0])
-        nc.sync.dma_start(weights[:, 1:2], w_by_partition[:, 1:2])
-        for b in range(1, C_BEFORE):
+
+        half = KB // 2
+        nc.sync.dma_start(weights[:, 0:2, 0:half], w_by_partition[:, 0:2, 0:half])
+        for b in range(half):
+            nc.sync.dma_start(blocks[b][:], table_by_block[b])
+        nc.sync.dma_start(weights[:, 0:2, half:KB], w_by_partition[:, 0:2, half:KB])
+        for b in range(half, C_BEFORE):
             nc.sync.dma_start(blocks[b][:], table_by_block[b])
 
         folded = held.tile([P, T], F32, name="folded", align_bytes=64)

import concourse.mybir as mybir

P = 128
S = 512
K = 512
KB = K // P
M = 128
E = 4
Q = 256
N = E * Q
T = 32
QC = Q // 16
C_BEFORE = 3
ROW_START = 256

FLOPS = 2 * K * M * N

BF16, F32, U16 = mybir.dt.bfloat16, mybir.dt.float32, mybir.dt.uint16
MULT = mybir.AluOpType.mult


def tile_gather_matmul_kernel(tc, table, w, c, offs, out):
    nc = tc.nc
    with (
        tc.tile_pool(name="held", bufs=1) as held,
        tc.psum_pool(name="psum", bufs=1) as psum,
    ):

        offsets = held.tile([P, N // 16], U16, name="offsets")
        nc.sync.dma_start(offsets[:], offs)

        weights = held.tile([P, E, KB, M], BF16, name="weights", align_bytes=ROW_START)
        w_by_partition = w.rearrange("e (p b) m -> p e b m", b=KB)

        table_by_block = table.rearrange("(p b) s -> b p s", b=KB)
        blocks = [held.tile([P, S], BF16, name=f"block{b}", align_bytes=ROW_START) for b in range(KB)]

        half = KB // 2
        nc.sync.dma_start(weights[:, 0:2, 0:half], w_by_partition[:, 0:2, 0:half])
        for b in range(half):
            nc.sync.dma_start(blocks[b][:], table_by_block[b])
        nc.sync.dma_start(weights[:, 0:2, half:KB], w_by_partition[:, 0:2, half:KB])
        for b in range(half, C_BEFORE):
            nc.sync.dma_start(blocks[b][:], table_by_block[b])

        folded = held.tile([P, T], F32, name="folded", align_bytes=64)
        c_rows = c.rearrange("o (a r) -> (o a) r", r=T)
        nc.sync.dma_start(folded[:], c_rows.partition_broadcast(P // T))

        for b in range(C_BEFORE, KB):
            nc.sync.dma_start(blocks[b][:], table_by_block[b])
        for e in range(2, E):
            nc.sync.dma_start(weights[:, e : e + 1], w_by_partition[:, e : e + 1])

        turned = held.tile([P, N // T], F32, name="turned", align_bytes=64)
        nc.vector.transpose(turned[:], folded[:])
        spread = held.tile([P, N // T, T], F32, name="spread", align_bytes=64)
        gains = held.tile([P, N], F32, name="gains", align_bytes=64)
        for e in range(E):
            rows = slice(e * (Q // T), (e + 1) * (Q // T))
            nc.scalar.copy(spread[:, rows], turned[:, rows].unsqueeze(2).to_broadcast([P, Q // T, T]))
            nc.vector.transpose(gains[:, e * Q : (e + 1) * Q], spread[:, rows].rearrange("p a r -> p (a r)"))

        banks = [psum.tile([P, Q], F32, name=f"bank{e}") for e in range(E)]
        for pair in range(0, E, 2):
            for b in range(KB):
                for e in (pair, pair + 1):
                    nc.tensor.matmul(
                        banks[e][:],
                        weights[:, e, b, :],
                        blocks[b][:].indirect(offsets[:, e * QC : (e + 1) * QC]),
                        start=(b == 0),
                        stop=(b == KB - 1),
                    )
            for e in (pair, pair + 1):
                scaled = held.tile([P, Q], F32, name=f"scaled{e}", align_bytes=ROW_START)
                width = Q // 2 if e == E - 1 else Q
                for first in range(0, Q, width):
                    columns = slice(e * Q + first, e * Q + first + width)
                    nc.vector.tensor_tensor(
                        scaled[:, first : first + width], banks[e][:, first : first + width], gains[:, columns], MULT
                    )
                    nc.sync.dma_start(out[:, columns], scaled[:, first : first + width])
